import numpy as np
import ml_dtypes


def mxq(x, axis, fmt="e4m3"):
    dtype, down = {"e4m3": (ml_dtypes.float8_e4m3fn, 7), "e5m2": (ml_dtypes.float8_e5m2, 14)}[fmt]
    v = np.moveaxis(np.asarray(x, np.float32).astype(ml_dtypes.bfloat16).astype(np.float64), axis, -1)
    blocks = v.reshape(v.shape[:-1] + (-1, 32))
    amax = np.abs(blocks).max(-1, keepdims=True)
    byte = np.maximum(np.where(amax > 0, np.frexp(amax)[1] - 1 + 127, 0) - down, 1)
    scale = np.exp2(byte - 127.0)
    codes = (blocks / scale).astype(np.float32).astype(dtype).astype(np.float64)
    return np.moveaxis((codes * scale).reshape(v.shape), -1, axis)


WIDE = False


def mx_kscale(k):
    if not WIDE:
        return np.ones(k)
    levels = np.array([10, -10, 5, -5, 0])
    if k % 512:
        return np.exp2(np.random.permutation(np.resize(levels, k // 32))).repeat(32)
    a = np.empty((k // 512, 16))
    for p in range(k // 512):
        a[p, :8] = np.random.permutation(np.resize(levels, 8))
        for g in range(8):
            far = levels[np.abs(levels - a[p, g]) >= 10]
            a[p, g + 8] = far[np.random.randint(len(far))]
    return np.exp2(a.ravel()).repeat(32)


def f64(x):
    return np.asarray(x).astype(np.float64)


def striped(idx):
    return np.tile(idx.reshape(-1, 16).T, (8, 1)).astype(np.uint16)


def unstriped(offs):
    return offs[:16].T.reshape(-1).astype(np.int64)


def pack_weight(w):
    k, n = w.shape
    w = f64(np.asarray(w, np.float32).astype(ml_dtypes.bfloat16)).reshape(k // 32, 32, n)
    amax = np.abs(w).max(1)
    byte = np.clip(np.where(amax > 0, np.frexp(amax)[1] - 1 + 127 - 7, 1), 1, 254)
    scaled = (w * np.exp2(127.0 - byte)[:, None, :]).reshape(k, n).astype(np.float32)
    words = np.ascontiguousarray(scaled.reshape(k // 512, 128, 4, n).transpose(0, 1, 3, 2)).astype(ml_dtypes.float8_e4m3fn).view(np.uint8)
    return words, np.ascontiguousarray(byte.astype(np.uint8).reshape(k // 512, 16, n))


def unpack_weight(words, scales):
    g, p, n, _ = words.shape
    vals = np.ascontiguousarray(words).view(ml_dtypes.float8_e4m3fn).astype(np.float64) * np.repeat(np.exp2(scales.astype(np.float64) - 127.0), 8, axis=1)[..., None]
    return vals.transpose(0, 1, 3, 2).reshape(g * 512, n)


def relu(v):
    return np.maximum(v, 0.0)


K, T, S, D, H, N, V, U = 512, 2048, 512, 2, 512, 256, 256, 512


def setup_inputs():
    n = np.random.standard_normal
    s = mx_kscale(K)[:, None]
    u = mx_kscale(H)
    packed_xT = pack_weight(n((K, T)) * s)
    return {
        "x_words": packed_xT[0],
        "x_scales": packed_xT[1],
        "w1": (n((K, H)) / np.sqrt(K) / s * u).astype(np.float32),
        "offm": (0.5 * n((H, S)) * u[:, None]).astype(np.float32),
        "k0": (n((H, N)) / np.sqrt(3 * H) / u[:, None]).astype(np.float32),
        "k1": (n((H, N)) / np.sqrt(3 * H) / u[:, None]).astype(np.float32),
        "k2": (n((H, N)) / np.sqrt(3 * H) / u[:, None]).astype(np.float32),
        "offs": striped(np.random.permutation(T)[:S]),
        "cell": striped(np.random.permutation(U)[:V]),
    }


def reference(x_words, x_scales, w1, offm, k0, k1, k2, offs, cell):
    xq = unpack_weight(x_words, x_scales)[:, unstriped(offs)]
    h = relu((mxq(f64(w1), 0, "e4m3").T @ xq) + f64(offm))
    pil = h.reshape(len(h), -1, D).max(axis=2)
    grid = np.zeros((H, S))
    grid[:, unstriped(cell)] = pil
    gridq = mxq(grid, 0, "e4m3")
    y0 = mxq(f64(k0), 0, "e4m3").T @ gridq
    y1 = mxq(f64(k1), 0, "e4m3").T @ gridq
    y2 = mxq(f64(k2), 0, "e4m3").T @ gridq
    return relu(y0 + np.pad(y1, ((0, 0), (1, 0)))[:, :S] + np.pad(y2, ((0, 0), (2, 0)))[:, :S])

@@ -1,0 +1,200 @@
+from contextlib import ExitStack
+
+import concourse.mybir as mybir
+
+K, T, S, H, N, V = 512, 2048, 512, 512, 256, 256
+FLOPS = 2 * K * H * S + 3 * 2 * H * N * S
+
+F32 = mybir.dt.float32
+BF16 = mybir.dt.bfloat16
+I32 = mybir.dt.int32
+U32 = mybir.dt.uint32
+U16 = mybir.dt.uint16
+U8 = mybir.dt.uint8
+FP8X4 = mybir.dt.float8_e4m3fn_x4
+ALU = mybir.AluOpType
+ACT = mybir.ActivationFunctionType
+
+P = 128
+PACK = 4
+HALF = 256
+WORD_PAD = 16
+BYTE_PAD = 64
+
+
+def tile_picked_ypillar_conv_p_kernel(
+    tc, x_words, x_scales, w1, offm, k0, k1, k2, offs, cell, out
+):
+    nc = tc.nc
+    taps = (k0, k1, k2)
+    with ExitStack() as ctx:
+        keep = ctx.enter_context(tc.tile_pool(name="keep", bufs=1))
+        psum = ctx.enter_context(tc.psum_pool(name="psum", bufs=1))
+
+        offs_sb = keep.tile([P, S // 16], U16, name="offs_sb")
+        cell_sb = keep.tile([P, V // 16], U16, name="cell_sb")
+        xs_all = keep.tile([P, T], U8, name="xs_all", tag="xs_then_off", align_bytes=64)
+        xw_all = keep.tile([P, T], I32, name="xw_all", align_bytes=64)
+        w1_raw = keep.tile([P, PACK, H], F32, name="w1_raw", tag="w1_then_k")
+        off_lo = keep.tile([P, 2, S], F32, name="off_lo")
+        k0_raw = keep.tile([P, PACK, N], F32, name="k0_raw", tag="kraw0", align_bytes=64)
+        grid = [keep.tile([P, S], F32, name="grid%d" % t) for t in range(PACK)]
+        g_words = keep.tile([P, WORD_PAD + S], I32, name="g_words", align_bytes=64)
+        g_scales = keep.tile([P, BYTE_PAD + S], U8, name="g_scales", align_bytes=64)
+
+        nc.vector.memset(xs_all[:].bitcast(I32), 0)
+        nc.sync.dma_start(offs_sb[:], offs)
+        nc.sync.dma_start(cell_sb[:], cell)
+        xs_rows = x_scales[0].bitcast(I32)
+        for q in range(4):
+            nc.scalar.dma_start(xs_all[32 * q : 32 * q + 4, :].bitcast(I32), xs_rows[4 * q : 4 * q + 4, :])
+        nc.sync.dma_start(w1_raw[:], w1.rearrange("(p j) c -> p j c", j=PACK))
+        nc.sync.dma_start(xw_all[:], x_words[0].rearrange("p n t -> p (n t)").bitcast(I32))
+        off_rows = offm.rearrange("(p t) s -> p t s", t=PACK)
+        k_rows = [k.rearrange("(p j) n -> p j n", j=PACK) for k in taps]
+        nc.sync.dma_start(off_lo[:], off_rows[:, 0:2, :])
+        nc.sync.dma_start(k0_raw[:], k_rows[0])
+
+        for t in range(PACK):
+            nc.vector.memset(grid[t][:], 0.0)
+        nc.vector.memset(g_words[:, 0:WORD_PAD], 0)
+        nc.vector.memset(g_scales[:].bitcast(I32), 0)
+
+        xs_pick = keep.tile([P, S], U8, name="xs_pick", align_bytes=64)
+        nc.vector.tensor_copy(xs_pick[:], xs_all[:].indirect(offs_sb[:]))
+        off_hi = keep.tile([P, 2, S], F32, name="off_hi", tag="xs_then_off", align_bytes=64)
+        nc.sync.dma_start(off_hi[:], off_rows[:, 2:4, :])
+        off_sb = [off_lo[:, 0, :], off_lo[:, 1, :], off_hi[:, 0, :], off_hi[:, 1, :]]
+
+        w1_bf = keep.tile([P, H * PACK], BF16, name="w1_bf", align_bytes=64)
+        w1_dst = w1_bf[:].rearrange("p (t m j) -> p m j t", t=PACK, j=PACK)
+        w1_src = w1_raw[:].rearrange("p j (m t) -> p m j t", t=PACK)
+        nc.vector.tensor_copy(w1_dst[:, 0:80], w1_src[:, 0:80])
+        nc.scalar.copy(w1_dst[:, 80:128], w1_src[:, 80:128])
+        k12_raw = keep.tile([P, 2, PACK, N], F32, name="k12_raw", tag="w1_then_k")
+        nc.sync.dma_start(k12_raw[:, 0], k_rows[1])
+        nc.sync.dma_start(k12_raw[:, 1], k_rows[2])
+        k_raw = [k0_raw[:], k12_raw[:, 0], k12_raw[:, 1]]
+        w1_words = keep.tile([P, H], U32, name="w1_words", align_bytes=64)
+        w1_scales = keep.tile([P, H], U8, name="w1_scales", align_bytes=64)
+        nc.vector.quantize_mx(out=w1_words[:].bitcast(FP8X4), scales=w1_scales[:], in_=w1_bf[:])
+
+        xw_pick = keep.tile([P, S], U32, name="xw_pick", align_bytes=64)
+        for hf in range(2):
+            nc.vector.tensor_copy(
+                xw_pick[:, hf * HALF : (hf + 1) * HALF],
+                xw_all[:].bitcast(U32).indirect(offs_sb[:, hf * 16 : (hf + 1) * 16]),
+            )
+
+        def layer(t, cols, tag):
+            acc = psum.tile([P, cols.stop - cols.start], F32, name="acc_" + tag, tag=tag)
+            m_cols = slice(t * P, (t + 1) * P)
+            nc.tensor.matmul_mx(
+                out=acc[:],
+                lhsT=w1_words[:, m_cols].bitcast(FP8X4),
+                lhsT_scale=w1_scales[:, m_cols],
+                rhs=xw_pick[:, cols].bitcast(FP8X4),
+                rhs_scale=xs_pick[:, cols],
+                start=True,
+                stop=True,
+            )
+            return acc
+
+        halves = [slice(0, HALF), slice(HALF, S)]
+        pieces = [[(layer(0, c, "b%d" % i), c) for i, c in enumerate(halves)]]
+        for t in range(1, PACK):
+            pieces.append([(layer(t, slice(0, S), "b%d" % (t + 1)), slice(0, S))])
+
+        k_words = keep.tile([P, 3, N], U32, name="k_words", align_bytes=64)
+        k_scales = keep.tile([P, 3, N], U8, name="k_scales", align_bytes=64)
+        k_bf = [keep.tile([P, N * PACK], BF16, name="kbf%d" % a, align_bytes=64) for a in range(3)]
+
+        def weave_tap(a):
+            nc.scalar.activation(
+                k_bf[a][:].rearrange("p (c i t) -> p c t i", i=4, t=PACK),
+                k_raw[a].rearrange("p t (c i) -> p c t i", i=4),
+                ACT.Copy,
+            )
+
+        def quantize_tap(a):
+            nc.vector.quantize_mx(out=k_words[:, a, :].bitcast(FP8X4), scales=k_scales[:, a, :], in_=k_bf[a][:])
+
+        hid = [keep.tile([P, S], F32, name="hid%d" % t) for t in range(PACK)]
+        pil = [keep.tile([P, V], F32, name="pil%d" % t) for t in range(PACK)]
+
+        def add_offsets(t):
+            for acc, cols in pieces[t]:
+                nc.vector.tensor_tensor(hid[t][:, cols], acc[:], off_sb[t][:, cols], ALU.add)
+
+        def pair_max(t):
+            pairs = hid[t][:].rearrange("p (v d) -> p v d", d=2)
+            nc.vector.scalar_tensor_tensor(pil[t][:], pairs[:, :, 0], 0.0, pairs[:, :, 1], ALU.max, ALU.max)
+
+        def scatter(t):
+            nc.vector.tensor_copy(grid[t][:].indirect(cell_sb[:]), pil[t][:])
+
+        weave_tap(0)
+        g_bf = keep.tile([P, PACK * S], BF16, name="g_bf", tag="kraw0", align_bytes=64)
+        g_planes = g_bf[:].rearrange("p (r t) -> p r t", t=PACK)
+
+        def weave_plane(t, cols):
+            nc.scalar.activation(g_planes[:, cols, t], grid[t][:, cols], ACT.Copy)
+
+        add_offsets(0)
+        pair_max(0)
+        add_offsets(1)
+        scatter(0)
+        weave_plane(0, slice(0, S))
+        weave_tap(1)
+        pair_max(1)
+        quantize_tap(0)
+        add_offsets(2)
+        scatter(1)
+        weave_plane(1, slice(0, S))
+        weave_tap(2)
+        pair_max(2)
+        quantize_tap(1)
+        add_offsets(3)
+        scatter(2)
+        weave_plane(2, slice(0, S))
+        pair_max(3)
+        quantize_tap(2)
+        scatter(3)
+
+        s_words = [keep.tile([P, S], U32, name="sw%d" % a, align_bytes=64) for a in (1, 2)]
+        s_scales = [keep.tile([P, S], U8, name="ss%d" % a, align_bytes=64) for a in (1, 2)]
+        gw = g_words[:].bitcast(U32)
+        for cols in halves:
+            weave_plane(3, cols)
+        for hf, cols in enumerate(halves):
+            c0, c1 = cols.start, cols.stop
+            nc.vector.quantize_mx(
+                out=gw[:, WORD_PAD + c0 : WORD_PAD + c1].bitcast(FP8X4),
+                scales=g_scales[:, BYTE_PAD + c0 : BYTE_PAD + c1],
+                in_=g_bf[:, PACK * c0 : PACK * c1],
+            )
+            moving = [(gw[:, WORD_PAD + c0 : WORD_PAD + c1], g_scales[:, BYTE_PAD + c0 : BYTE_PAD + c1])]
+            for a in (1, 2):
+                nc.vector.tensor_copy(s_words[a - 1][:, cols], gw[:, WORD_PAD + c0 - a : WORD_PAD + c1 - a])
+                nc.vector.tensor_copy(s_scales[a - 1][:, cols], g_scales[:, BYTE_PAD + c0 - a : BYTE_PAD + c1 - a])
+                moving.append((s_words[a - 1][:, cols], s_scales[a - 1][:, cols]))
+            accs = [psum.tile([P, HALF], F32, name="y%d%d" % (hf, m), tag="b%d" % (5 + m if hf == 0 else (7 if m == 0 else 0))) for m in range(2)]
+            for a in range(3):
+                for m in range(2):
+                    m_cols = slice(m * P, (m + 1) * P)
+                    nc.tensor.matmul_mx(
+                        out=accs[m][:],
+                        lhsT=k_words[:, a, m_cols].bitcast(FP8X4),
+                        lhsT_scale=k_scales[:, a, m_cols],
+                        rhs=moving[a][0].bitcast(FP8X4),
+                        rhs_scale=moving[a][1],
+                        start=(a == 0),
+                        stop=(a == 2),
+                    )
+            for m in range(2):
+                res = keep.tile([P, HALF], F32, name="res%d%d" % (hf, m))
+                if hf == 1 and m == 1:
+                    nc.vector.tensor_scalar_max(res[:], accs[m][:], 0.0)
+                else:
+                    nc.scalar.activation(res[:], accs[m][:], ACT.Relu)
+                nc.sync.dma_start(out[m * P : (m + 1) * P, cols], res[:])

@@ -20,6 +20,7 @@ PACK = 4
 HALF = 256
 WORD_PAD = 16
 BYTE_PAD = 64
+SLOT = (2, 0, 1, 3)
 
 
 def tile_picked_ypillar_conv_p_kernel(
@@ -29,70 +30,83 @@ def tile_picked_ypillar_conv_p_kernel(
     taps = (k0, k1, k2)
     with ExitStack() as ctx:
         keep = ctx.enter_context(tc.tile_pool(name="keep", bufs=1))
+        shared = ctx.enter_context(tc.tile_pool(name="shared", bufs=1))
         psum = ctx.enter_context(tc.psum_pool(name="psum", bufs=1))
 
         offs_sb = keep.tile([P, S // 16], U16, name="offs_sb")
         cell_sb = keep.tile([P, V // 16], U16, name="cell_sb")
-        xs_all = keep.tile([P, T], U8, name="xs_all", tag="xs_then_off", align_bytes=64)
-        xw_all = keep.tile([P, T], I32, name="xw_all", align_bytes=64)
-        w1_raw = keep.tile([P, PACK, H], F32, name="w1_raw", tag="w1_then_k")
+        xs_all = keep.tile([P, T], U8, name="xs_all", align_bytes=64)
+        xw_all = keep.tile([P, T], I32, name="xw_all", tag="xw_then_w1", align_bytes=64)
+        w1_raw = shared.tile([P, PACK, H], F32, name="w1_raw", offset=0, align_bytes=64)
         off_lo = keep.tile([P, 2, S], F32, name="off_lo")
-        k0_raw = keep.tile([P, PACK, N], F32, name="k0_raw", tag="kraw0", align_bytes=64)
-        grid = [keep.tile([P, S], F32, name="grid%d" % t) for t in range(PACK)]
+        k0_raw = keep.tile([P, PACK, N], F32, name="k0_raw")
+        grid = [keep.tile([P, S], F32, name="grid%d" % t, tag="grid%d" % t, align_bytes=64) for t in range(PACK)]
         g_words = keep.tile([P, WORD_PAD + S], I32, name="g_words", align_bytes=64)
         g_scales = keep.tile([P, BYTE_PAD + S], U8, name="g_scales", align_bytes=64)
 
+        xs_land = keep.tile([P, T // 4], I32, name="xs_land", tag="land_then_k1")
         nc.vector.memset(xs_all[:].bitcast(I32), 0)
-        nc.sync.dma_start(offs_sb[:], offs)
-        nc.sync.dma_start(cell_sb[:], cell)
         xs_rows = x_scales[0].bitcast(I32)
         for q in range(4):
-            nc.scalar.dma_start(xs_all[32 * q : 32 * q + 4, :].bitcast(I32), xs_rows[4 * q : 4 * q + 4, :])
+            nc.sync.dma_start(xs_land[32 * q : 32 * q + 4, :], xs_rows[4 * q : 4 * q + 4, :])
+        nc.sync.dma_start(offs_sb[:], offs)
         nc.sync.dma_start(w1_raw[:], w1.rearrange("(p j) c -> p j c", j=PACK))
         nc.sync.dma_start(xw_all[:], x_words[0].rearrange("p n t -> p (n t)").bitcast(I32))
-        off_rows = offm.rearrange("(p t) s -> p t s", t=PACK)
+        nc.sync.dma_start(cell_sb[:], cell)
         k_rows = [k.rearrange("(p j) n -> p j n", j=PACK) for k in taps]
-        nc.sync.dma_start(off_lo[:], off_rows[:, 0:2, :])
+        nc.sync.dma_start(off_lo[:], offm.rearrange("(p u t) s -> p u t s", u=2, t=2)[:, :, 0, :])
         nc.sync.dma_start(k0_raw[:], k_rows[0])
 
-        for t in range(PACK):
-            nc.vector.memset(grid[t][:], 0.0)
-        nc.vector.memset(g_words[:, 0:WORD_PAD], 0)
-        nc.vector.memset(g_scales[:].bitcast(I32), 0)
 
+        for q in range(4):
+            nc.vector.tensor_copy(xs_all[32 * q : 32 * q + 4, :].bitcast(I32), xs_land[32 * q : 32 * q + 4, :])
         xs_pick = keep.tile([P, S], U8, name="xs_pick", align_bytes=64)
         nc.vector.tensor_copy(xs_pick[:], xs_all[:].indirect(offs_sb[:]))
-        off_hi = keep.tile([P, 2, S], F32, name="off_hi", tag="xs_then_off", align_bytes=64)
-        nc.sync.dma_start(off_hi[:], off_rows[:, 2:4, :])
-        off_sb = [off_lo[:, 0, :], off_lo[:, 1, :], off_hi[:, 0, :], off_hi[:, 1, :]]
+        k1_raw = keep.tile([P, PACK, N], F32, name="k1_raw", tag="land_then_k1")
+        nc.sync.dma_start(k1_raw[:], k_rows[1])
 
-        w1_bf = keep.tile([P, H * PACK], BF16, name="w1_bf", align_bytes=64)
-        w1_dst = w1_bf[:].rearrange("p (t m j) -> p m j t", t=PACK, j=PACK)
-        w1_src = w1_raw[:].rearrange("p j (m t) -> p m j t", t=PACK)
-        nc.vector.tensor_copy(w1_dst[:, 0:80], w1_src[:, 0:80])
-        nc.scalar.copy(w1_dst[:, 80:128], w1_src[:, 80:128])
-        k12_raw = keep.tile([P, 2, PACK, N], F32, name="k12_raw", tag="w1_then_k")
-        nc.sync.dma_start(k12_raw[:, 0], k_rows[1])
-        nc.sync.dma_start(k12_raw[:, 1], k_rows[2])
-        k_raw = [k0_raw[:], k12_raw[:, 0], k12_raw[:, 1]]
-        w1_words = keep.tile([P, H], U32, name="w1_words", align_bytes=64)
-        w1_scales = keep.tile([P, H], U8, name="w1_scales", align_bytes=64)
-        nc.vector.quantize_mx(out=w1_words[:].bitcast(FP8X4), scales=w1_scales[:], in_=w1_bf[:])
+        w1_src = w1_raw[:].rearrange("p j (m u e) -> p e m j u", u=2, e=2)
+        w1_bf = [keep.tile([P, H * 2], BF16, name="w1bf%d" % e, tag="w1bf%d" % e, align_bytes=64) for e in range(2)]
+        for e in range(2):
+            nc.scalar.copy(w1_bf[e][:].rearrange("p (u m j) -> p m j u", u=2, j=PACK), w1_src[:, e])
+        off_hi = shared.tile([P, 2, S], F32, name="off_hi", offset=0, align_bytes=64)
+        k2_raw = shared.tile([P, PACK, N], F32, name="k2_raw", offset=4096, align_bytes=64)
+        nc.sync.dma_start(off_hi[:], offm.rearrange("(p u t) s -> p u t s", u=2, t=2)[:, :, 1, :])
+        nc.sync.dma_start(k2_raw[:], k_rows[2])
+        off_sb = [off_lo[:, 1, :], off_lo[:, 0, :], off_hi[:, 0, :], off_hi[:, 1, :]]
+        k_raw = [k0_raw[:], k1_raw[:], k2_raw[:]]
+        w1_words = []
+        w1_scales = [keep.tile([P, HALF], U8, name="w1s%d" % e, align_bytes=64) for e in range(2)]
 
-        xw_pick = keep.tile([P, S], U32, name="xw_pick", align_bytes=64)
+        def quantize_w1(e):
+            tag = ("w1w0", "xw_then_w1")[e]
+            w1_words.append(keep.tile([P, HALF], U32, name="w1w%d" % e, tag=tag, align_bytes=64))
+            nc.vector.quantize_mx(out=w1_words[e][:].bitcast(FP8X4), scales=w1_scales[e][:], in_=w1_bf[e][:])
+
+        quantize_w1(0)
+
+        xw_pick = keep.tile([P, S], U32, name="xw_pick", tag="w1bf0", align_bytes=64)
         for hf in range(2):
             nc.vector.tensor_copy(
                 xw_pick[:, hf * HALF : (hf + 1) * HALF],
                 xw_all[:].bitcast(U32).indirect(offs_sb[:, hf * 16 : (hf + 1) * 16]),
             )
 
+        for t in range(PACK):
+            nc.vector.memset(grid[t][:], 0.0)
+        spare = keep.tile([P, 1], F32, name="spare")
+        nc.scalar.activation(spare[:], grid[0][:, 0:1], ACT.Copy)
+        nc.vector.memset(g_words[:, 0:WORD_PAD], 0)
+        nc.vector.memset(g_scales[:].bitcast(I32), 0)
+
         def layer(t, cols, tag):
             acc = psum.tile([P, cols.stop - cols.start], F32, name="acc_" + tag, tag=tag)
-            m_cols = slice(t * P, (t + 1) * P)
+            u, e = divmod(SLOT[t], 2)
+            m_cols = slice(u * P, (u + 1) * P)
             nc.tensor.matmul_mx(
                 out=acc[:],
-                lhsT=w1_words[:, m_cols].bitcast(FP8X4),
-                lhsT_scale=w1_scales[:, m_cols],
+                lhsT=w1_words[e][:, m_cols].bitcast(FP8X4),
+                lhsT_scale=w1_scales[e][:, m_cols],
                 rhs=xw_pick[:, cols].bitcast(FP8X4),
                 rhs_scale=xs_pick[:, cols],
                 start=True,
@@ -102,10 +116,11 @@ def tile_picked_ypillar_conv_p_kernel(
 
         halves = [slice(0, HALF), slice(HALF, S)]
         pieces = [[(layer(0, c, "b%d" % i), c) for i, c in enumerate(halves)]]
+        quantize_w1(1)
         for t in range(1, PACK):
             pieces.append([(layer(t, slice(0, S), "b%d" % (t + 1)), slice(0, S))])
 
-        k_words = keep.tile([P, 3, N], U32, name="k_words", align_bytes=64)
+        k_words = []
         k_scales = keep.tile([P, 3, N], U8, name="k_scales", align_bytes=64)
         k_bf = [keep.tile([P, N * PACK], BF16, name="kbf%d" % a, align_bytes=64) for a in range(3)]
 
@@ -117,55 +132,70 @@ def tile_picked_ypillar_conv_p_kernel(
             )
 
         def quantize_tap(a):
-            nc.vector.quantize_mx(out=k_words[:, a, :].bitcast(FP8X4), scales=k_scales[:, a, :], in_=k_bf[a][:])
+            k_words.append(keep.tile([P, N], U32, name="kw%d" % a, tag=("step2", "step3", "grid0")[a], align_bytes=64))
+            nc.vector.quantize_mx(out=k_words[a][:].bitcast(FP8X4), scales=k_scales[:, a, :], in_=k_bf[a][:])
 
-        hid = [keep.tile([P, S], F32, name="hid%d" % t) for t in range(PACK)]
-        pil = [keep.tile([P, V], F32, name="pil%d" % t) for t in range(PACK)]
+        hid = []
 
         def add_offsets(t):
+            hid.append(keep.tile([P, S], F32, name="hid%d" % t, tag="step%d" % t, align_bytes=64))
             for acc, cols in pieces[t]:
                 nc.vector.tensor_tensor(hid[t][:, cols], acc[:], off_sb[t][:, cols], ALU.add)
 
-        def pair_max(t):
-            pairs = hid[t][:].rearrange("p (v d) -> p v d", d=2)
-            nc.vector.scalar_tensor_tensor(pil[t][:], pairs[:, :, 0], 0.0, pairs[:, :, 1], ALU.max, ALU.max)
+        def pair_max(t, tag, lo=0, hi=V):
+            pil = keep.tile([P, hi - lo], F32, name="pil%d_%d" % (t, lo), tag=tag, align_bytes=64)
+            pairs = hid[t][:, 2 * lo : 2 * hi].rearrange("p (v d) -> p v d", d=2)
+            nc.vector.scalar_tensor_tensor(pil[:], pairs[:, :, 0], 0.0, pairs[:, :, 1], ALU.max, ALU.max)
+            return pil
 
-        def scatter(t):
-            nc.vector.tensor_copy(grid[t][:].indirect(cell_sb[:]), pil[t][:])
+        def scatter(t, pil, lo=0, hi=V):
+            nc.vector.tensor_copy(grid[t][:].indirect(cell_sb[:, lo // 16 : hi // 16]), pil[:])
 
-        weave_tap(0)
-        g_bf = keep.tile([P, PACK * S], BF16, name="g_bf", tag="kraw0", align_bytes=64)
+        for a in range(3):
+            weave_tap(a)
+        g_bf = shared.tile([P, PACK * S], BF16, name="g_bf", offset=4096, align_bytes=64)
         g_planes = g_bf[:].rearrange("p (r t) -> p r t", t=PACK)
 
         def weave_plane(t, cols):
-            nc.scalar.activation(g_planes[:, cols, t], grid[t][:, cols], ACT.Copy)
+            nc.scalar.activation(g_planes[:, cols, SLOT[t]], grid[t][:, cols], ACT.Copy)
 
         add_offsets(0)
-        pair_max(0)
+        pil = pair_max(0, "step2")
         add_offsets(1)
-        scatter(0)
+        scatter(0, pil)
         weave_plane(0, slice(0, S))
-        weave_tap(1)
-        pair_max(1)
-        quantize_tap(0)
+        pil = pair_max(1, "step3")
         add_offsets(2)
-        scatter(1)
+        scatter(1, pil)
         weave_plane(1, slice(0, S))
-        weave_tap(2)
-        pair_max(2)
-        quantize_tap(1)
+        pil = pair_max(2, "pil2")
+        quantize_tap(0)
         add_offsets(3)
-        scatter(2)
+        scatter(2, pil)
         weave_plane(2, slice(0, S))
-        pair_max(3)
+        pil_a = pair_max(3, "grid0", 0, V // 2)
+        pil_b = pair_max(3, "pil3b", V // 2, V)
+        quantize_tap(1)
+        scatter(3, pil_a, 0, V // 2)
         quantize_tap(2)
-        scatter(3)
+        warm = psum.tile([P, S], F32, name="warm", tag="b2")
+        for width in (S, S, HALF):
+            nc.tensor.matmul_mx(
+                out=warm[:, 0:width],
+                lhsT=k_words[2][:, 0:P].bitcast(FP8X4),
+                lhsT_scale=k_scales[:, 2, 0:P],
+                rhs=xw_pick[:, 0:width].bitcast(FP8X4),
+                rhs_scale=xs_pick[:, 0:width],
+                start=True,
+                stop=True,
+            )
+        scatter(3, pil_b, V // 2, V)
 
         s_words = [keep.tile([P, S], U32, name="sw%d" % a, align_bytes=64) for a in (1, 2)]
         s_scales = [keep.tile([P, S], U8, name="ss%d" % a, align_bytes=64) for a in (1, 2)]
         gw = g_words[:].bitcast(U32)
-        for cols in halves:
-            weave_plane(3, cols)
+        nc.vector.tensor_copy(g_planes[:, halves[0], 3], grid[3][:, halves[0]])
+        weave_plane(3, halves[1])
         for hf, cols in enumerate(halves):
             c0, c1 = cols.start, cols.stop
             nc.vector.quantize_mx(
@@ -184,7 +214,7 @@ def tile_picked_ypillar_conv_p_kernel(
                     m_cols = slice(m * P, (m + 1) * P)
                     nc.tensor.matmul_mx(
                         out=accs[m][:],
-                        lhsT=k_words[:, a, m_cols].bitcast(FP8X4),
+                        lhsT=k_words[a][:, m_cols].bitcast(FP8X4),
                         lhsT_scale=k_scales[:, a, m_cols],
                         rhs=moving[a][0].bitcast(FP8X4),
                         rhs_scale=moving[a][1],
@@ -197,4 +227,5 @@ def tile_picked_ypillar_conv_p_kernel(
                     nc.vector.tensor_scalar_max(res[:], accs[m][:], 0.0)
                 else:
                     nc.scalar.activation(res[:], accs[m][:], ACT.Relu)
-                nc.sync.dma_start(out[m * P : (m + 1) * P, cols], res[:])
+                queue = nc.scalar if (hf == 1 and m == 0) else nc.sync
+                queue.dma_start(out[m * P : (m + 1) * P, cols], res[:])

@@ -39,12 +39,12 @@ def tile_picked_ypillar_conv_p_kernel(
         xw_all = keep.tile([P, T], I32, name="xw_all", tag="xw_then_w1", align_bytes=64)
         w1_raw = shared.tile([P, PACK, H], F32, name="w1_raw", offset=0, align_bytes=64)
         off_lo = keep.tile([P, 2, S], F32, name="off_lo")
-        k0_raw = keep.tile([P, PACK, N], F32, name="k0_raw")
+        k0_raw = keep.tile([P, PACK, N], F32, name="k0_raw", tag="k0_raw", align_bytes=64)
         grid = [keep.tile([P, S], F32, name="grid%d" % t, tag="grid%d" % t, align_bytes=64) for t in range(PACK)]
         g_words = keep.tile([P, WORD_PAD + S], I32, name="g_words", align_bytes=64)
         g_scales = keep.tile([P, BYTE_PAD + S], U8, name="g_scales", align_bytes=64)
 
-        xs_land = keep.tile([P, T // 4], I32, name="xs_land", tag="land_then_k1")
+        xs_land = keep.tile([P, T // 4], I32, name="xs_land", tag="land_then_k1", align_bytes=64)
         nc.vector.memset(xs_all[:].bitcast(I32), 0)
         xs_rows = x_scales[0].bitcast(I32)
         for q in range(4):
@@ -62,7 +62,7 @@ def tile_picked_ypillar_conv_p_kernel(
             nc.vector.tensor_copy(xs_all[32 * q : 32 * q + 4, :].bitcast(I32), xs_land[32 * q : 32 * q + 4, :])
         xs_pick = keep.tile([P, S], U8, name="xs_pick", align_bytes=64)
         nc.vector.tensor_copy(xs_pick[:], xs_all[:].indirect(offs_sb[:]))
-        k1_raw = keep.tile([P, PACK, N], F32, name="k1_raw", tag="land_then_k1")
+        k1_raw = keep.tile([P, PACK, N], F32, name="k1_raw", tag="land_then_k1", align_bytes=64)
         nc.sync.dma_start(k1_raw[:], k_rows[1])
 
         w1_src = w1_raw[:].rearrange("p j (m u e) -> p e m j u", u=2, e=2)
@@ -132,7 +132,7 @@ def tile_picked_ypillar_conv_p_kernel(
             )
 
         def quantize_tap(a):
-            k_words.append(keep.tile([P, N], U32, name="kw%d" % a, tag=("step2", "step3", "grid0")[a], align_bytes=64))
+            k_words.append(keep.tile([P, N], U32, name="kw%d" % a, tag=("pil0", "k0_raw", "grid0")[a], align_bytes=64))
             nc.vector.quantize_mx(out=k_words[a][:].bitcast(FP8X4), scales=k_scales[:, a, :], in_=k_bf[a][:])
 
         hid = []
@@ -141,6 +141,16 @@ def tile_picked_ypillar_conv_p_kernel(
             hid.append(keep.tile([P, S], F32, name="hid%d" % t, tag="step%d" % t, align_bytes=64))
             for acc, cols in pieces[t]:
                 nc.vector.tensor_tensor(hid[t][:, cols], acc[:], off_sb[t][:, cols], ALU.add)
+
+        def leave_psum(t):
+            acc, cols = pieces[t][0]
+            prod = keep.tile([P, S], F32, name="prod%d" % t)
+            nc.scalar.copy(prod[:], acc[:])
+            return prod
+
+        def add_offsets_beside(t, prod):
+            hid.append(keep.tile([P, S], F32, name="hid%d" % t, tag="step1", align_bytes=64))
+            nc.gpsimd.tensor_tensor(hid[t][:], prod[:], off_sb[t], ALU.add)
 
         def pair_max(t, tag, lo=0, hi=V):
             pil = keep.tile([P, hi - lo], F32, name="pil%d_%d" % (t, lo), tag=tag, align_bytes=64)
@@ -151,8 +161,10 @@ def tile_picked_ypillar_conv_p_kernel(
         def scatter(t, pil, lo=0, hi=V):
             nc.vector.tensor_copy(grid[t][:].indirect(cell_sb[:, lo // 16 : hi // 16]), pil[:])
 
-        for a in range(3):
-            weave_tap(a)
+        weave_tap(0)
+        prods = {t: leave_psum(t) for t in (2, 3)}
+        weave_tap(1)
+        weave_tap(2)
         g_bf = shared.tile([P, PACK * S], BF16, name="g_bf", offset=4096, align_bytes=64)
         g_planes = g_bf[:].rearrange("p (r t) -> p r t", t=PACK)
 
@@ -160,22 +172,22 @@ def tile_picked_ypillar_conv_p_kernel(
             nc.scalar.activation(g_planes[:, cols, SLOT[t]], grid[t][:, cols], ACT.Copy)
 
         add_offsets(0)
-        pil = pair_max(0, "step2")
+        pil = pair_max(0, "pil0")
         add_offsets(1)
         scatter(0, pil)
         weave_plane(0, slice(0, S))
-        pil = pair_max(1, "step3")
-        add_offsets(2)
+        pil = pair_max(1, "k0_raw")
+        quantize_tap(0)
+        add_offsets_beside(2, prods[2])
         scatter(1, pil)
         weave_plane(1, slice(0, S))
-        pil = pair_max(2, "pil2")
-        quantize_tap(0)
-        add_offsets(3)
+        pil = pair_max(2, "land_then_k1")
+        quantize_tap(1)
+        add_offsets_beside(3, prods[3])
         scatter(2, pil)
         weave_plane(2, slice(0, S))
         pil_a = pair_max(3, "grid0", 0, V // 2)
         pil_b = pair_max(3, "pil3b", V // 2, V)
-        quantize_tap(1)
         scatter(3, pil_a, 0, V // 2)
         quantize_tap(2)
         warm = psum.tile([P, S], F32, name="warm", tag="b2")

@@ -38,7 +38,7 @@ def tile_picked_ypillar_conv_p_kernel(
         xs_all = keep.tile([P, T], U8, name="xs_all", align_bytes=64)
         xw_all = keep.tile([P, T], I32, name="xw_all", tag="xw_then_w1", align_bytes=64)
         w1_raw = shared.tile([P, PACK, H], F32, name="w1_raw", offset=0, align_bytes=64)
-        off_lo = keep.tile([P, 2, S], F32, name="off_lo")
+        off_lo = [keep.tile([P, S], F32, name="off_lo%d" % i) for i in range(2)]
         k0_raw = keep.tile([P, PACK, N], F32, name="k0_raw", tag="k0_raw", align_bytes=64)
         grid = [keep.tile([P, S], F32, name="grid%d" % t, tag="grid%d" % t, align_bytes=64) for t in range(PACK)]
         g_words = keep.tile([P, WORD_PAD + S], I32, name="g_words", align_bytes=64)
@@ -48,14 +48,17 @@ def tile_picked_ypillar_conv_p_kernel(
         nc.vector.memset(xs_all[:].bitcast(I32), 0)
         xs_rows = x_scales[0].bitcast(I32)
         for q in range(4):
-            nc.sync.dma_start(xs_land[32 * q : 32 * q + 4, :], xs_rows[4 * q : 4 * q + 4, :])
+            queue = nc.scalar if q < 2 else nc.sync
+            queue.dma_start(xs_land[32 * q : 32 * q + 4, :], xs_rows[4 * q : 4 * q + 4, :])
         nc.sync.dma_start(offs_sb[:], offs)
         nc.sync.dma_start(w1_raw[:], w1.rearrange("(p j) c -> p j c", j=PACK))
         nc.sync.dma_start(xw_all[:], x_words[0].rearrange("p n t -> p (n t)").bitcast(I32))
         nc.sync.dma_start(cell_sb[:], cell)
         k_rows = [k.rearrange("(p j) n -> p j n", j=PACK) for k in taps]
-        nc.sync.dma_start(off_lo[:], offm.rearrange("(p u t) s -> p u t s", u=2, t=2)[:, :, 0, :])
+        off_rows = offm.rearrange("(p t) s -> t p s", t=PACK)
+        nc.sync.dma_start(off_lo[0][:], off_rows[SLOT[0]])
         nc.sync.dma_start(k0_raw[:], k_rows[0])
+        nc.sync.dma_start(off_lo[1][:], off_rows[SLOT[1]])
 
 
         for q in range(4):
@@ -69,11 +72,12 @@ def tile_picked_ypillar_conv_p_kernel(
         w1_bf = [keep.tile([P, H * 2], BF16, name="w1bf%d" % e, tag="w1bf%d" % e, align_bytes=64) for e in range(2)]
         for e in range(2):
             nc.scalar.copy(w1_bf[e][:].rearrange("p (u m j) -> p m j u", u=2, j=PACK), w1_src[:, e])
-        off_hi = shared.tile([P, 2, S], F32, name="off_hi", offset=0, align_bytes=64)
+        off_hi = [shared.tile([P, S], F32, name="off_hi%d" % i, offset=2048 * i, align_bytes=64) for i in range(2)]
         k2_raw = shared.tile([P, PACK, N], F32, name="k2_raw", offset=4096, align_bytes=64)
-        nc.sync.dma_start(off_hi[:], offm.rearrange("(p u t) s -> p u t s", u=2, t=2)[:, :, 1, :])
         nc.sync.dma_start(k2_raw[:], k_rows[2])
-        off_sb = [off_lo[:, 1, :], off_lo[:, 0, :], off_hi[:, 0, :], off_hi[:, 1, :]]
+        nc.sync.dma_start(off_hi[0][:], off_rows[SLOT[2]])
+        nc.sync.dma_start(off_hi[1][:], off_rows[SLOT[3]])
+        off_sb = [off_lo[0][:], off_lo[1][:], off_hi[0][:], off_hi[1][:]]
         k_raw = [k0_raw[:], k1_raw[:], k2_raw[:]]
         w1_words = []
         w1_scales = [keep.tile([P, HALF], U8, name="w1s%d" % e, align_bytes=64) for e in range(2)]
@@ -122,17 +126,26 @@ def tile_picked_ypillar_conv_p_kernel(
 
         k_words = []
         k_scales = keep.tile([P, 3, N], U8, name="k_scales", align_bytes=64)
-        k_bf = [keep.tile([P, N * PACK], BF16, name="kbf%d" % a, align_bytes=64) for a in range(3)]
+        k_bf = {}
 
         def weave_tap(a):
-            nc.scalar.activation(
-                k_bf[a][:].rearrange("p (c i t) -> p c t i", i=4, t=PACK),
-                k_raw[a].rearrange("p t (c i) -> p c t i", i=4),
-                ACT.Copy,
-            )
+            k_bf[a] = keep.tile([P, N * PACK], BF16, name="kbf%d" % a, tag=("kbf0", "step0", "kbf2")[a], align_bytes=64)
+            dst = k_bf[a][:].rearrange("p (c i t) -> p c t i", i=4, t=PACK)
+            src = k_raw[a].rearrange("p t (c i) -> p c t i", i=4)
+            if a == 1:
+                nc.gpsimd.tensor_scalar(
+                    k_bf[a][:].rearrange("p (c t) -> p c t", t=PACK),
+                    k_raw[a].rearrange("p t c -> p c t"),
+                    1.0,
+                    0.0,
+                    ALU.mult,
+                    ALU.add,
+                )
+            else:
+                nc.scalar.activation(dst, src, ACT.Copy)
 
         def quantize_tap(a):
-            k_words.append(keep.tile([P, N], U32, name="kw%d" % a, tag=("pil0", "k0_raw", "grid0")[a], align_bytes=64))
+            k_words.append(keep.tile([P, N], U32, name="kw%d" % a, tag=("pil0", "prod2", "step1")[a], align_bytes=64))
             nc.vector.quantize_mx(out=k_words[a][:].bitcast(FP8X4), scales=k_scales[:, a, :], in_=k_bf[a][:])
 
         hid = []
@@ -144,7 +157,7 @@ def tile_picked_ypillar_conv_p_kernel(
 
         def leave_psum(t):
             acc, cols = pieces[t][0]
-            prod = keep.tile([P, S], F32, name="prod%d" % t)
+            prod = keep.tile([P, S], F32, name="prod%d" % t, tag="prod%d" % t, align_bytes=64)
             nc.scalar.copy(prod[:], acc[:])
             return prod
 
@@ -163,7 +176,6 @@ def tile_picked_ypillar_conv_p_kernel(
 
         weave_tap(0)
         prods = {t: leave_psum(t) for t in (2, 3)}
-        weave_tap(1)
         weave_tap(2)
         g_bf = shared.tile([P, PACK * S], BF16, name="g_bf", offset=4096, align_bytes=64)
         g_planes = g_bf[:].rearrange("p (r t) -> p r t", t=PACK)
@@ -173,6 +185,7 @@ def tile_picked_ypillar_conv_p_kernel(
 
         add_offsets(0)
         pil = pair_max(0, "pil0")
+        weave_tap(1)
         add_offsets(1)
         scatter(0, pil)
         weave_plane(0, slice(0, S))
@@ -181,7 +194,7 @@ def tile_picked_ypillar_conv_p_kernel(
         add_offsets_beside(2, prods[2])
         scatter(1, pil)
         weave_plane(1, slice(0, S))
-        pil = pair_max(2, "land_then_k1")
+        pil = pair_max(2, "pil2")
         quantize_tap(1)
         add_offsets_beside(3, prods[3])
         scatter(2, pil)

from contextlib import ExitStack

import concourse.mybir as mybir

K, T, S, H, N, V = 512, 2048, 512, 512, 256, 256
FLOPS = 2 * K * H * S + 3 * 2 * H * N * S

F32 = mybir.dt.float32
BF16 = mybir.dt.bfloat16
I32 = mybir.dt.int32
U32 = mybir.dt.uint32
U16 = mybir.dt.uint16
U8 = mybir.dt.uint8
FP8X4 = mybir.dt.float8_e4m3fn_x4
ALU = mybir.AluOpType
ACT = mybir.ActivationFunctionType

P = 128
PACK = 4
HALF = 256
WORD_PAD = 16
BYTE_PAD = 64
SLOT = (2, 0, 1, 3)


def tile_picked_ypillar_conv_p_kernel(
    tc, x_words, x_scales, w1, offm, k0, k1, k2, offs, cell, out
):
    nc = tc.nc
    taps = (k0, k1, k2)
    with ExitStack() as ctx:
        keep = ctx.enter_context(tc.tile_pool(name="keep", bufs=1))
        shared = ctx.enter_context(tc.tile_pool(name="shared", bufs=1))
        psum = ctx.enter_context(tc.psum_pool(name="psum", bufs=1))

        offs_sb = keep.tile([P, S // 16], U16, name="offs_sb")
        cell_sb = keep.tile([P, V // 16], U16, name="cell_sb")
        xs_all = keep.tile([P, T], U8, name="xs_all", align_bytes=64)
        xw_all = keep.tile([P, T], I32, name="xw_all", tag="xw_then_w1", align_bytes=64)
        w1_raw = shared.tile([P, PACK, H], F32, name="w1_raw", offset=0, align_bytes=64)
        off_lo = [keep.tile([P, S], F32, name="off_lo%d" % i) for i in range(2)]
        k0_raw = keep.tile([P, PACK, N], F32, name="k0_raw", tag="k0_raw", align_bytes=64)
        grid = [keep.tile([P, S], F32, name="grid%d" % t, tag="grid%d" % t, align_bytes=64) for t in range(PACK)]
        g_words = keep.tile([P, WORD_PAD + S], I32, name="g_words", align_bytes=64)
        g_scales = keep.tile([P, BYTE_PAD + S], U8, name="g_scales", align_bytes=64)

        xs_land = keep.tile([P, T // 4], I32, name="xs_land", tag="land_then_k1", align_bytes=64)
        nc.vector.memset(xs_all[:].bitcast(I32), 0)
        xs_rows = x_scales[0].bitcast(I32)
        for q in range(4):
            queue = nc.scalar if q < 2 else nc.sync
            queue.dma_start(xs_land[32 * q : 32 * q + 4, :], xs_rows[4 * q : 4 * q + 4, :])
        nc.sync.dma_start(offs_sb[:], offs)
        nc.sync.dma_start(w1_raw[:], w1.rearrange("(p j) c -> p j c", j=PACK))
        nc.sync.dma_start(xw_all[:], x_words[0].rearrange("p n t -> p (n t)").bitcast(I32))
        nc.sync.dma_start(cell_sb[:], cell)
        k_rows = [k.rearrange("(p j) n -> p j n", j=PACK) for k in taps]
        off_rows = offm.rearrange("(p t) s -> t p s", t=PACK)
        nc.sync.dma_start(off_lo[0][:], off_rows[SLOT[0]])
        nc.sync.dma_start(k0_raw[:], k_rows[0])
        nc.sync.dma_start(off_lo[1][:], off_rows[SLOT[1]])


        for q in range(4):
            nc.vector.tensor_copy(xs_all[32 * q : 32 * q + 4, :].bitcast(I32), xs_land[32 * q : 32 * q + 4, :])
        xs_pick = keep.tile([P, S], U8, name="xs_pick", align_bytes=64)
        nc.vector.tensor_copy(xs_pick[:], xs_all[:].indirect(offs_sb[:]))
        k1_raw = keep.tile([P, PACK, N], F32, name="k1_raw", tag="land_then_k1", align_bytes=64)
        nc.sync.dma_start(k1_raw[:], k_rows[1])

        w1_src = w1_raw[:].rearrange("p j (m u e) -> p e m j u", u=2, e=2)
        w1_bf = [keep.tile([P, H * 2], BF16, name="w1bf%d" % e, tag="w1bf%d" % e, align_bytes=64) for e in range(2)]
        for e in range(2):
            nc.scalar.copy(w1_bf[e][:].rearrange("p (u m j) -> p m j u", u=2, j=PACK), w1_src[:, e])
        off_hi = [shared.tile([P, S], F32, name="off_hi%d" % i, offset=2048 * i, align_bytes=64) for i in range(2)]
        k2_raw = shared.tile([P, PACK, N], F32, name="k2_raw", offset=4096, align_bytes=64)
        nc.sync.dma_start(k2_raw[:], k_rows[2])
        nc.sync.dma_start(off_hi[0][:], off_rows[SLOT[2]])
        nc.sync.dma_start(off_hi[1][:], off_rows[SLOT[3]])
        off_sb = [off_lo[0][:], off_lo[1][:], off_hi[0][:], off_hi[1][:]]
        k_raw = [k0_raw[:], k1_raw[:], k2_raw[:]]
        w1_words = []
        w1_scales = [keep.tile([P, HALF], U8, name="w1s%d" % e, align_bytes=64) for e in range(2)]

        def quantize_w1(e):
            tag = ("w1w0", "xw_then_w1")[e]
            w1_words.append(keep.tile([P, HALF], U32, name="w1w%d" % e, tag=tag, align_bytes=64))
            nc.vector.quantize_mx(out=w1_words[e][:].bitcast(FP8X4), scales=w1_scales[e][:], in_=w1_bf[e][:])

        quantize_w1(0)

        xw_pick = keep.tile([P, S], U32, name="xw_pick", tag="w1bf0", align_bytes=64)
        for hf in range(2):
            nc.vector.tensor_copy(
                xw_pick[:, hf * HALF : (hf + 1) * HALF],
                xw_all[:].bitcast(U32).indirect(offs_sb[:, hf * 16 : (hf + 1) * 16]),
            )

        for t in range(PACK):
            nc.vector.memset(grid[t][:], 0.0)
        spare = keep.tile([P, 1], F32, name="spare")
        nc.scalar.activation(spare[:], grid[0][:, 0:1], ACT.Copy)
        nc.vector.memset(g_words[:, 0:WORD_PAD], 0)
        nc.vector.memset(g_scales[:].bitcast(I32), 0)

        def layer(t, cols, tag):
            acc = psum.tile([P, cols.stop - cols.start], F32, name="acc_" + tag, tag=tag)
            u, e = divmod(SLOT[t], 2)
            m_cols = slice(u * P, (u + 1) * P)
            nc.tensor.matmul_mx(
                out=acc[:],
                lhsT=w1_words[e][:, m_cols].bitcast(FP8X4),
                lhsT_scale=w1_scales[e][:, m_cols],
                rhs=xw_pick[:, cols].bitcast(FP8X4),
                rhs_scale=xs_pick[:, cols],
                start=True,
                stop=True,
            )
            return acc

        halves = [slice(0, HALF), slice(HALF, S)]
        pieces = [[(layer(0, c, "b%d" % i), c) for i, c in enumerate(halves)]]
        quantize_w1(1)
        for t in range(1, PACK):
            pieces.append([(layer(t, slice(0, S), "b%d" % (t + 1)), slice(0, S))])

        k_words = []
        k_scales = keep.tile([P, 3, N], U8, name="k_scales", align_bytes=64)
        k_bf = {}

        def weave_tap(a):
            k_bf[a] = keep.tile([P, N * PACK], BF16, name="kbf%d" % a, tag=("kbf0", "step0", "kbf2")[a], align_bytes=64)
            dst = k_bf[a][:].rearrange("p (c i t) -> p c t i", i=4, t=PACK)
            src = k_raw[a].rearrange("p t (c i) -> p c t i", i=4)
            if a == 1:
                nc.gpsimd.tensor_scalar(
                    k_bf[a][:].rearrange("p (c t) -> p c t", t=PACK),
                    k_raw[a].rearrange("p t c -> p c t"),
                    1.0,
                    0.0,
                    ALU.mult,
                    ALU.add,
                )
            else:
                nc.scalar.activation(dst, src, ACT.Copy)

        def quantize_tap(a):
            k_words.append(keep.tile([P, N], U32, name="kw%d" % a, tag=("pil0", "prod2", "step1")[a], align_bytes=64))
            nc.vector.quantize_mx(out=k_words[a][:].bitcast(FP8X4), scales=k_scales[:, a, :], in_=k_bf[a][:])

        hid = []

        def add_offsets(t):
            hid.append(keep.tile([P, S], F32, name="hid%d" % t, tag="step%d" % t, align_bytes=64))
            for acc, cols in pieces[t]:
                nc.vector.tensor_tensor(hid[t][:, cols], acc[:], off_sb[t][:, cols], ALU.add)

        def leave_psum(t):
            acc, cols = pieces[t][0]
            prod = keep.tile([P, S], F32, name="prod%d" % t, tag="prod%d" % t, align_bytes=64)
            nc.scalar.copy(prod[:], acc[:])
            return prod

        def add_offsets_beside(t, prod):
            hid.append(keep.tile([P, S], F32, name="hid%d" % t, tag="step1", align_bytes=64))
            nc.gpsimd.tensor_tensor(hid[t][:], prod[:], off_sb[t], ALU.add)

        def pair_max(t, tag, lo=0, hi=V):
            pil = keep.tile([P, hi - lo], F32, name="pil%d_%d" % (t, lo), tag=tag, align_bytes=64)
            pairs = hid[t][:, 2 * lo : 2 * hi].rearrange("p (v d) -> p v d", d=2)
            nc.vector.scalar_tensor_tensor(pil[:], pairs[:, :, 0], 0.0, pairs[:, :, 1], ALU.max, ALU.max)
            return pil

        def scatter(t, pil, lo=0, hi=V):
            nc.vector.tensor_copy(grid[t][:].indirect(cell_sb[:, lo // 16 : hi // 16]), pil[:])

        weave_tap(0)
        prods = {t: leave_psum(t) for t in (2, 3)}
        weave_tap(2)
        g_bf = shared.tile([P, PACK * S], BF16, name="g_bf", offset=4096, align_bytes=64)
        g_planes = g_bf[:].rearrange("p (r t) -> p r t", t=PACK)

        def weave_plane(t, cols):
            nc.scalar.activation(g_planes[:, cols, SLOT[t]], grid[t][:, cols], ACT.Copy)

        add_offsets(0)
        pil = pair_max(0, "pil0")
        weave_tap(1)
        add_offsets(1)
        scatter(0, pil)
        weave_plane(0, slice(0, S))
        pil = pair_max(1, "k0_raw")
        quantize_tap(0)
        add_offsets_beside(2, prods[2])
        scatter(1, pil)
        weave_plane(1, slice(0, S))
        pil = pair_max(2, "pil2")
        quantize_tap(1)
        add_offsets_beside(3, prods[3])
        scatter(2, pil)
        weave_plane(2, slice(0, S))
        pil_a = pair_max(3, "grid0", 0, V // 2)
        pil_b = pair_max(3, "pil3b", V // 2, V)
        scatter(3, pil_a, 0, V // 2)
        quantize_tap(2)
        warm = psum.tile([P, S], F32, name="warm", tag="b2")
        for width in (S, S, HALF):
            nc.tensor.matmul_mx(
                out=warm[:, 0:width],
                lhsT=k_words[2][:, 0:P].bitcast(FP8X4),
                lhsT_scale=k_scales[:, 2, 0:P],
                rhs=xw_pick[:, 0:width].bitcast(FP8X4),
                rhs_scale=xs_pick[:, 0:width],
                start=True,
                stop=True,
            )
        scatter(3, pil_b, V // 2, V)

        s_words = [keep.tile([P, S], U32, name="sw%d" % a, align_bytes=64) for a in (1, 2)]
        s_scales = [keep.tile([P, S], U8, name="ss%d" % a, align_bytes=64) for a in (1, 2)]
        gw = g_words[:].bitcast(U32)
        nc.vector.tensor_copy(g_planes[:, halves[0], 3], grid[3][:, halves[0]])
        weave_plane(3, halves[1])
        for hf, cols in enumerate(halves):
            c0, c1 = cols.start, cols.stop
            nc.vector.quantize_mx(
                out=gw[:, WORD_PAD + c0 : WORD_PAD + c1].bitcast(FP8X4),
                scales=g_scales[:, BYTE_PAD + c0 : BYTE_PAD + c1],
                in_=g_bf[:, PACK * c0 : PACK * c1],
            )
            moving = [(gw[:, WORD_PAD + c0 : WORD_PAD + c1], g_scales[:, BYTE_PAD + c0 : BYTE_PAD + c1])]
            for a in (1, 2):
                nc.vector.tensor_copy(s_words[a - 1][:, cols], gw[:, WORD_PAD + c0 - a : WORD_PAD + c1 - a])
                nc.vector.tensor_copy(s_scales[a - 1][:, cols], g_scales[:, BYTE_PAD + c0 - a : BYTE_PAD + c1 - a])
                moving.append((s_words[a - 1][:, cols], s_scales[a - 1][:, cols]))
            accs = [psum.tile([P, HALF], F32, name="y%d%d" % (hf, m), tag="b%d" % (5 + m if hf == 0 else (7 if m == 0 else 0))) for m in range(2)]
            for a in range(3):
                for m in range(2):
                    m_cols = slice(m * P, (m + 1) * P)
                    nc.tensor.matmul_mx(
                        out=accs[m][:],
                        lhsT=k_words[a][:, m_cols].bitcast(FP8X4),
                        lhsT_scale=k_scales[:, a, m_cols],
                        rhs=moving[a][0].bitcast(FP8X4),
                        rhs_scale=moving[a][1],
                        start=(a == 0),
                        stop=(a == 2),
                    )
            for m in range(2):
                res = keep.tile([P, HALF], F32, name="res%d%d" % (hf, m))
                if hf == 1 and m == 1:
                    nc.vector.tensor_scalar_max(res[:], accs[m][:], 0.0)
                else:
                    nc.scalar.activation(res[:], accs[m][:], ACT.Relu)
                queue = nc.scalar if (hf == 1 and m == 0) else nc.sync
                queue.dma_start(out[m * P : (m + 1) * P, cols], res[:])
